import numpy as np
import ml_dtypes


def mxq(x, axis, fmt="e4m3"):
    dtype, down = {"e4m3": (ml_dtypes.float8_e4m3fn, 7), "e5m2": (ml_dtypes.float8_e5m2, 14)}[fmt]
    v = np.moveaxis(np.asarray(x, np.float32).astype(ml_dtypes.bfloat16).astype(np.float64), axis, -1)
    blocks = v.reshape(v.shape[:-1] + (-1, 32))
    amax = np.abs(blocks).max(-1, keepdims=True)
    byte = np.maximum(np.where(amax > 0, np.frexp(amax)[1] - 1 + 127, 0) - down, 1)
    scale = np.exp2(byte - 127.0)
    codes = (blocks / scale).astype(np.float32).astype(dtype).astype(np.float64)
    return np.moveaxis((codes * scale).reshape(v.shape), -1, axis)


WIDE = False


def mx_kscale(k):
    if not WIDE:
        return np.ones(k)
    levels = np.array([10, -10, 5, -5, 0])
    if k % 512:
        return np.exp2(np.random.permutation(np.resize(levels, k // 32))).repeat(32)
    a = np.empty((k // 512, 16))
    for p in range(k // 512):
        a[p, :8] = np.random.permutation(np.resize(levels, 8))
        for g in range(8):
            far = levels[np.abs(levels - a[p, g]) >= 10]
            a[p, g + 8] = far[np.random.randint(len(far))]
    return np.exp2(a.ravel()).repeat(32)


BF16 = ml_dtypes.bfloat16


def bf(x):
    return np.asarray(x, np.float32).astype(BF16)


def f64(x):
    return np.asarray(x).astype(np.float64)


E2M1 = np.array([0.0, 0.5, 1.0, 1.5, 2.0, 3.0, 4.0, 6.0, -0.0, -0.5, -1.0, -1.5, -2.0, -3.0, -4.0, -6.0])


def pack_weight(w, fmt):
    k, n = w.shape
    w = f64(bf(w)).reshape(k // 32, 32, n)
    amax = np.abs(w).max(1)
    if fmt == "e4m3":
        byte = np.frexp(amax)[1] - 1 + 127 - 7
    else:
        mant, ex = np.frexp(amax / 6.0)
        byte = np.where(mant > 0.5, ex, ex - 1) + 127
    byte = np.clip(np.where(amax > 0, byte, 1), 1, 254)
    scaled = (w * np.exp2(127.0 - byte)[:, None, :]).reshape(k, n).astype(np.float32)
    by_word = np.ascontiguousarray(scaled.reshape(k // 512, 128, 4, n).transpose(0, 1, 3, 2))
    if fmt == "e4m3":
        words = by_word.astype(ml_dtypes.float8_e4m3fn).view(np.uint8)
    else:
        c = by_word.astype(ml_dtypes.float4_e2m1fn).view(np.uint8) & 0xF
        words = c[..., 0::2] | (c[..., 1::2] << 4)
    return np.ascontiguousarray(words), np.ascontiguousarray(byte.astype(np.uint8).reshape(k // 512, 16, n))


def unpack_weight(words, scales, fmt):
    g, p, n, _ = words.shape
    if fmt == "e4m3":
        vals = np.ascontiguousarray(words).view(ml_dtypes.float8_e4m3fn).astype(np.float64)
    else:
        nib = np.empty((g, p, n, 4), np.uint8)
        nib[..., 0::2] = words & 0xF
        nib[..., 1::2] = words >> 4
        vals = E2M1[nib]
    vals = vals * np.repeat(np.exp2(scales.astype(np.float64) - 127.0), 8, axis=1)[..., None]
    return vals.transpose(0, 1, 3, 2).reshape(g * 512, n)
def pack4(w):
    words, scales = pack_weight(w, "e2m1")
    return words.reshape(words.shape[0], 128, -1), scales


def unpack4(words, scales):
    return unpack_weight(words.reshape(words.shape[0], 128, -1, 2), scales, "e2m1")


M, D, L, H, N, W = 1024, 2048, 1024, 512, 2048, 8


def setup_inputs():
    a = mx_kscale(D)
    b = mx_kscale(L)
    t = mx_kscale(H)
    x = bf(np.random.standard_normal((M, D)) * a)
    wq = bf(np.random.standard_normal((D, H)) / np.sqrt(D) / H ** 0.25 / a[:, None] * t)
    u_words, u_scales = pack4(np.random.standard_normal((L, H)) / np.sqrt(L) / H ** 0.25 * b[:, None] / t)
    c_words, c_scales = pack4(np.random.standard_normal((L, N)) / b[:, None])
    lme = bf(0.5 + 0.3 * np.random.standard_normal(M))
    vnorm = bf(np.abs(1 + 0.3 * np.random.standard_normal(N)))
    return {"x": x, "wq": wq, "u_words": u_words, "u_scales": u_scales,
            "c_words": c_words, "c_scales": c_scales, "lme": lme, "vnorm": vnorm}


def reference(x, wq, u_words, u_scales, c_words, c_scales, lme, vnorm):
    query = mxq(f64(x), 1, "e4m3") @ mxq(f64(wq), 0, "e4m3")
    keys = unpack4(u_words, u_scales).T @ unpack4(c_words, c_scales)
    logits = mxq(query, 1, "e4m3") @ mxq(keys, 0, "e4m3")
    prob = np.exp(logits - f64(lme)[:, None])
    return prob.reshape(M // W, W, N).sum(1) * f64(vnorm)

@@ -1,0 +1,385 @@
+from contextlib import ExitStack
+
+import concourse.mybir as mybir
+from concourse.masks import make_identity
+
+M, D, L, H, N, W = 1024, 2048, 1024, 512, 2048, 8
+FLOPS = 2 * (M * D * H + H * L * N + M * H * N)
+
+F32 = mybir.dt.float32
+BF16 = mybir.dt.bfloat16
+I32 = mybir.dt.int32
+U32 = mybir.dt.uint32
+U8 = mybir.dt.uint8
+FP8X4 = mybir.dt.float8_e4m3fn_x4
+FP4X4 = mybir.dt.float4_e2m1fn_x4
+ACT = mybir.ActivationFunctionType
+ALU = mybir.AluOpType
+
+P = 128
+PACK = 4
+K_PASS = P * PACK
+D_PASSES = D // K_PASS
+L_PASSES = L // K_PASS
+CHUNK = 512
+CHUNKS = N // CHUNK
+
+
+def tile_heavy_hitter_scores_s12_kernel(tc, x, wq, u_words, u_scales, c_words, c_scales, lme, vnorm, out):
+    nc = tc.nc
+    with ExitStack() as ctx:
+        keep = ctx.enter_context(tc.tile_pool(name="keep", bufs=1))
+        stage = ctx.enter_context(tc.tile_pool(name="stage", bufs=3))
+        ahead = ctx.enter_context(tc.tile_pool(name="ahead", bufs=4))
+        probs = ctx.enter_context(tc.tile_pool(name="probs", bufs=6))
+        psum = ctx.enter_context(tc.psum_pool(name="psum", bufs=8))
+        ctx.enter_context(tc.manual_schedule())
+
+        def kept(name, shape, dtype):
+            return keep.tile(shape, dtype, name=name, align_bytes=64)
+
+        def new_bank():
+            return psum.tile([P, CHUNK], F32, name="bank", tag="bank")
+
+        ident = kept("ident", [P, P], F32)
+        lme_sb = kept("lme_sb", [P, W], BF16)
+        neg_lme = kept("neg_lme", [P, W], F32)
+        x_sb = [kept("x_sb%d" % i, [P, D], BF16) for i in range(W)]
+        wq_raw = [kept("wq_raw%d" % g, [P, PACK, H], BF16) for g in range(D_PASSES)]
+        wq_codes = [kept("wq_codes%d" % g, [P, H], U32) for g in range(D_PASSES)]
+        wq_scale = [kept("wq_scale%d" % g, [P, H], U8) for g in range(D_PASSES)]
+        u_raw = kept("u_raw", [P, L_PASSES, 2 * H], U8)
+        u_scale_raw = kept("u_scale_raw", [P, L_PASSES, H], U8)
+        u_codes = kept("u_codes", [P, L_PASSES, 2 * H], U8)
+        u_scale = kept("u_scale", [P, L_PASSES, H], U8)
+        c_codes = [kept("c_codes%d" % c, [P, L_PASSES, 2 * CHUNK], U8) for c in range(CHUNKS)]
+        c_scale = kept("c_scale", [P, L_PASSES, N], U8)
+        key_codes = [kept("key_codes%d" % c, [P, CHUNK], U32) for c in range(CHUNKS)]
+        key_scale = [kept("key_scale%d" % c, [P, CHUNK], U8) for c in range(CHUNKS)]
+        total = [kept("total%d" % c, [P, CHUNK], F32) for c in range(CHUNKS)]
+        vnorm_sb = kept("vnorm_sb", [P, N], BF16)
+
+        x_tiles = x.rearrange("(w i) d -> i w d", i=W)
+        u_scale_rows = u_scales.rearrange("g (q r) n -> r q g n", r=4)
+        c_scale_rows = c_scales.rearrange("g (q r) n -> r q g n", r=4)
+
+        def load_x(i):
+            nc.sync.dma_start(out=x_sb[i][:], in_=x_tiles[i])
+
+        def load_wq(g):
+            rows = wq[g * K_PASS : (g + 1) * K_PASS, :]
+            nc.sync.dma_start(out=wq_raw[g][:], in_=rows.rearrange("(p j) h -> p j h", j=PACK))
+
+        def load_c(c):
+            cols = c_words.rearrange("g p b -> p g b")[:, :, 2 * CHUNK * c : 2 * CHUNK * (c + 1)]
+            nc.sync.dma_start(out=c_codes[c][:].bitcast(I32), in_=cols.bitcast(I32))
+
+        def load_scale_rows(queue, plane, rows, r):
+            queue.dma_start(out=plane[r:P:32, :, :].bitcast(I32), in_=rows[r].bitcast(I32))
+
+        def quantize(codes, scales, values):
+            nc.vector.quantize_mx(out=codes[:].bitcast(FP8X4), scales=scales[:], in_=values[:])
+
+        def sort_u():
+            nc.vector.tensor_copy(
+                out=u_codes[:].bitcast(I32).rearrange("p g (t b w) -> p g t b w", t=PACK, w=2),
+                in_=u_raw[:].bitcast(I32).rearrange("p g (b t w) -> p g t b w", t=PACK, w=2),
+            )
+            nc.vector.tensor_copy(
+                out=u_scale[:].bitcast(I32).rearrange("p g (t b) -> p g t b", t=PACK),
+                in_=u_scale_raw[:].bitcast(I32).rearrange("p g (b t) -> p g t b", t=PACK),
+            )
+
+        V, S = nc.vector.tensor_copy, nc.scalar.copy
+        held = {}
+
+        def group_wq(g, copy=V):
+            grouped = stage.tile([P, H * PACK], BF16, name="wq_grouped", align_bytes=64, bufs=2)
+            copy(
+                out=grouped[:].rearrange("p (t b i j) -> p t b j i", t=PACK, i=4, j=PACK),
+                in_=wq_raw[g][:].rearrange("p j (b t i) -> p t b j i", t=PACK, i=4),
+            )
+            held["wq", g] = grouped
+
+        def quantize_wq(g):
+            quantize(wq_codes[g], wq_scale[g], held["wq", g])
+
+        def sort_x(i):
+            words = keep.tile([P, D // 2], F32, name="x_sorted%d" % i)
+            nc.vector.tensor_copy(
+                out=words[:].rearrange("p (g u w) -> p g u w", g=D_PASSES, u=2),
+                in_=x_sb[i][:].bitcast(F32).rearrange("p (g w u) -> p g u w", g=D_PASSES, u=2),
+            )
+            held["sorted", i] = words
+
+        def transpose_x(i):
+            held["x", i] = ahead.tile([P, D], BF16, name="x_grouped", align_bytes=64)
+            for half in range(2):
+                bank = new_bank()
+                for k in range(4):
+                    g, u = 2 * half + k // 2, k % 2
+                    if ("sorted", i) in held:
+                        words = held["sorted", i][:, (2 * g + u) * P : (2 * g + u + 1) * P]
+                    else:
+                        words = x_sb[i][:].bitcast(F32)[:, 256 * g + u : 256 * (g + 1) : 2]
+                    nc.tensor.transpose(bank[:, k * P : (k + 1) * P], words, ident[:])
+                held["x_bank", i, half] = bank
+
+        def copy_x(i, half, copy):
+            half_words = D // 4
+            copy(
+                out=held["x", i][:].bitcast(F32)[:, half * half_words : (half + 1) * half_words].rearrange("p (g q u) -> p g q u", g=2, u=2),
+                in_=held["x_bank", i, half][:].rearrange("p (g u q) -> p g q u", g=2, u=2),
+            )
+
+        def quantize_x(i):
+            codes = ahead.tile([P, D // PACK], U32, name="x_codes", align_bytes=64)
+            scales = ahead.tile([P, D // PACK], U8, name="x_scale", align_bytes=64)
+            quantize(codes, scales, held["x", i])
+            held["x_operand", i] = codes, scales
+
+        def keys_piece(c, piece, copy=S):
+            if piece == 0:
+                held["keys", c] = stage.tile([P, CHUNK * PACK], BF16, name="key_grouped", align_bytes=64, bufs=2)
+            bank = new_bank()
+            n0 = c * CHUNK + piece * P
+            for t in range(PACK):
+                for g in range(L_PASSES):
+                    nc.tensor.matmul_mx(
+                        out=bank[:, t * P : (t + 1) * P],
+                        lhsT=u_codes[:, g, 2 * P * t : 2 * P * (t + 1)].bitcast(FP4X4),
+                        lhsT_scale=u_scale[:, g, P * t : P * (t + 1)],
+                        rhs=c_codes[c][:, g, 2 * P * piece : 2 * P * (piece + 1)].bitcast(FP4X4),
+                        rhs_scale=c_scale[:, g, n0 : n0 + P],
+                        start=(g == 0),
+                        stop=(g == L_PASSES - 1),
+                    )
+            copy(
+                out=held["keys", c][:, piece * K_PASS : (piece + 1) * K_PASS].rearrange("p (n t) -> p n t", t=PACK),
+                in_=bank[:].rearrange("p (t n) -> p n t", t=PACK),
+            )
+
+        def keys_chunk(c, copies=(S, S, S, S)):
+            for piece in range(CHUNK // P):
+                keys_piece(c, piece, copies[piece])
+
+        def quantize_keys(c):
+            quantize(key_codes[c], key_scale[c], held["keys", c])
+
+        def query_tile(i, copy):
+            codes, scales = held["x_operand", i]
+            bank = new_bank()
+            for t in range(PACK):
+                for g in range(D_PASSES):
+                    nc.tensor.matmul_mx(
+                        out=bank[:, t * P : (t + 1) * P],
+                        lhsT=wq_codes[g][:, P * t : P * (t + 1)].bitcast(FP8X4),
+                        lhsT_scale=wq_scale[g][:, P * t : P * (t + 1)],
+                        rhs=codes[:, P * g : P * (g + 1)].bitcast(FP8X4),
+                        rhs_scale=scales[:, P * g : P * (g + 1)],
+                        start=(g == 0),
+                        stop=(g == D_PASSES - 1),
+                    )
+            grouped = stage.tile([P, K_PASS], BF16, name="query_grouped", align_bytes=64)
+            copy(
+                out=grouped[:].rearrange("p (q t) -> p q t", t=PACK),
+                in_=bank[:].rearrange("p (t q) -> p q t", t=PACK),
+            )
+            held["query", i] = grouped
+
+        def quantize_query(i):
+            codes = keep.tile([P, P], U32, name="query_codes%d" % i, align_bytes=64)
+            scales = keep.tile([P, P], U8, name="query_scale%d" % i, align_bytes=64)
+            quantize(codes, scales, held["query", i])
+            held["query_operand", i] = codes, scales
+
+        def probabilities(i, c):
+            codes, scales = held["query_operand", i]
+            bank = new_bank()
+            nc.tensor.matmul_mx(
+                out=bank[:],
+                lhsT=codes[:].bitcast(FP8X4),
+                lhsT_scale=scales[:],
+                rhs=key_codes[c][:].bitcast(FP8X4),
+                rhs_scale=key_scale[c][:],
+                start=True,
+                stop=True,
+            )
+            if i == 0:
+                nc.scalar.activation(out=total[c][:], in_=bank[:], func=ACT.Exp, bias=neg_lme[:, i : i + 1])
+                return
+            prob = probs.tile([P, CHUNK], F32, name="prob")
+            nc.scalar.activation(out=prob[:], in_=bank[:], func=ACT.Exp, bias=neg_lme[:, i : i + 1])
+            held["prob", i, c] = prob
+
+        def add(i, c):
+            if i > 0:
+                nc.vector.tensor_tensor(out=total[c][:], in0=total[c][:], in1=held["prob", i, c][:], op=ALU.add)
+
+        def finish(c):
+            cols = slice(c * CHUNK, (c + 1) * CHUNK)
+            result = probs.tile([P, CHUNK], F32, name="result", bufs=4)
+            nc.vector.tensor_tensor(out=result[:], in0=total[c][:], in1=vnorm_sb[:, cols], op=ALU.mult)
+            nc.sync.dma_start(out=out[:, cols], in_=result[:])
+
+        nc.gpsimd.memset(u_scale_raw[:].bitcast(I32), 0)
+        nc.vector.memset(c_scale[:].bitcast(I32), 0)
+        make_identity(nc, ident[:])
+        nc.sync.dma_start(out=lme_sb[:], in_=lme.rearrange("(w i) -> w i", i=W))
+        for r in range(4):
+            load_scale_rows(nc.sync, u_scale_raw, u_scale_rows, r)
+        load_scale_rows(nc.sync, c_scale, c_scale_rows, 0)
+        nc.sync.dma_start(out=u_raw[:].bitcast(I32), in_=u_words.rearrange("g p b -> p g b").bitcast(I32))
+        load_x(0)
+        for r in range(1, 4):
+            load_scale_rows(nc.sync, c_scale, c_scale_rows, r)
+        load_c(0)
+        load_wq(0)
+        load_c(1)
+        load_wq(1)
+        load_c(2)
+        load_wq(2)
+        load_wq(3)
+        load_c(3)
+        load_x(1)
+        load_x(2)
+        load_x(3)
+        load_x(4)
+        load_x(5)
+        load_x(6)
+        load_x(7)
+        nc.sync.dma_start(out=vnorm_sb[:], in_=vnorm.partition_broadcast(P))
+        nc.scalar.activation(out=neg_lme[:], in_=lme_sb[:], func=ACT.Copy, scale=-1.0)
+        transpose_x(0)
+        copy_x(0, 0, S)
+        copy_x(0, 1, S)
+        sort_u()
+        quantize_x(0)
+        keys_chunk(0)
+        group_wq(0, V)
+        group_wq(1, V)
+        quantize_wq(0)
+        keys_chunk(1)
+        quantize_wq(1)
+        group_wq(2, V)
+        quantize_keys(0)
+        quantize_wq(2)
+        keys_chunk(2)
+        group_wq(3, V)
+        quantize_keys(1)
+        quantize_wq(3)
+        transpose_x(1)
+        copy_x(1, 0, S)
+        copy_x(1, 1, S)
+        keys_chunk(3)
+        quantize_keys(2)
+        query_tile(0, V)
+        quantize_x(1)
+        quantize_keys(3)
+        quantize_query(0)
+        transpose_x(2)
+        copy_x(2, 0, S)
+        copy_x(2, 1, S)
+        query_tile(1, V)
+        quantize_x(2)
+        quantize_query(1)
+        probabilities(0, 0)
+        add(0, 0)
+        probabilities(0, 1)
+        add(0, 1)
+        probabilities(0, 2)
+        add(0, 2)
+        probabilities(0, 3)
+        add(0, 3)
+        transpose_x(3)
+        copy_x(3, 0, S)
+        copy_x(3, 1, S)
+        query_tile(2, V)
+        quantize_x(3)
+        quantize_query(2)
+        probabilities(1, 0)
+        add(1, 0)
+        probabilities(1, 1)
+        add(1, 1)
+        probabilities(1, 2)
+        add(1, 2)
+        probabilities(1, 3)
+        add(1, 3)
+        transpose_x(4)
+        copy_x(4, 0, S)
+        copy_x(4, 1, S)
+        query_tile(3, V)
+        quantize_x(4)
+        quantize_query(3)
+        probabilities(2, 0)
+        add(2, 0)
+        probabilities(2, 1)
+        add(2, 1)
+        probabilities(2, 2)
+        add(2, 2)
+        probabilities(2, 3)
+        add(2, 3)
+        transpose_x(5)
+        copy_x(5, 0, S)
+        copy_x(5, 1, S)
+        query_tile(4, V)
+        quantize_x(5)
+        quantize_query(4)
+        probabilities(3, 0)
+        add(3, 0)
+        probabilities(3, 1)
+        add(3, 1)
+        probabilities(3, 2)
+        add(3, 2)
+        probabilities(3, 3)
+        add(3, 3)
+        transpose_x(6)
+        copy_x(6, 0, S)
+        copy_x(6, 1, S)
+        query_tile(5, V)
+        quantize_x(6)
+        quantize_query(5)
+        probabilities(4, 0)
+        add(4, 0)
+        probabilities(4, 1)
+        add(4, 1)
+        probabilities(4, 2)
+        add(4, 2)
+        probabilities(4, 3)
+        add(4, 3)
+        transpose_x(7)
+        copy_x(7, 0, S)
+        copy_x(7, 1, S)
+        query_tile(6, V)
+        quantize_x(7)
+        quantize_query(6)
+        probabilities(5, 0)
+        add(5, 0)
+        probabilities(5, 1)
+        add(5, 1)
+        probabilities(5, 2)
+        add(5, 2)
+        probabilities(5, 3)
+        add(5, 3)
+        query_tile(7, S)
+        quantize_query(7)
+        probabilities(6, 0)
+        add(6, 0)
+        probabilities(6, 1)
+        add(6, 1)
+        probabilities(6, 2)
+        add(6, 2)
+        probabilities(6, 3)
+        add(6, 3)
+        probabilities(7, 0)
+        add(7, 0)
+        probabilities(7, 1)
+        add(7, 1)
+        finish(0)
+        probabilities(7, 2)
+        add(7, 2)
+        finish(1)
+        probabilities(7, 3)
+        add(7, 3)
+        finish(2)
+        finish(3)

@@ -18,53 +18,65 @@ ALU = mybir.AluOpType
 
 P = 128
 PACK = 4
+RUN = 4
 K_PASS = P * PACK
 D_PASSES = D // K_PASS
 L_PASSES = L // K_PASS
 CHUNK = 512
 CHUNKS = N // CHUNK
+HALF = CHUNK // 2
+SCALE_ROWS = 4
+TENSOR_CHUNK = CHUNKS - 1
+FIRST_RUN = range(1, 5)
+SECOND_RUN = range(5, W)
+LEAD = 2
+EARLY_SUMS = 2
 
 
 def tile_heavy_hitter_scores_s12_kernel(tc, x, wq, u_words, u_scales, c_words, c_scales, lme, vnorm, out):
     nc = tc.nc
+    on_vector, on_scalar = nc.vector.tensor_copy, nc.scalar.copy
     with ExitStack() as ctx:
         keep = ctx.enter_context(tc.tile_pool(name="keep", bufs=1))
-        stage = ctx.enter_context(tc.tile_pool(name="stage", bufs=3))
-        ahead = ctx.enter_context(tc.tile_pool(name="ahead", bufs=4))
-        probs = ctx.enter_context(tc.tile_pool(name="probs", bufs=6))
-        psum = ctx.enter_context(tc.psum_pool(name="psum", bufs=8))
+        shared = ctx.enter_context(tc.tile_pool(name="shared", bufs=W))
+        stage = ctx.enter_context(tc.tile_pool(name="stage", bufs=2))
+        turned = ctx.enter_context(tc.tile_pool(name="turned", bufs=6))
+        probs = ctx.enter_context(tc.tile_pool(name="probs", bufs=5))
+        psum = ctx.enter_context(tc.psum_pool(name="psum", bufs=7))
+        sum_pool = ctx.enter_context(tc.psum_pool(name="sum_pool", bufs=1))
         ctx.enter_context(tc.manual_schedule())
 
         def kept(name, shape, dtype):
             return keep.tile(shape, dtype, name=name, align_bytes=64)
 
+        def kept_operand(name, columns):
+            return kept(name + "_codes", [P, columns], U32), kept(name + "_scale", [P, columns], U8)
+
         def new_bank():
-            return psum.tile([P, CHUNK], F32, name="bank", tag="bank")
+            return psum.tile([P, CHUNK], F32, name="bank")
 
         ident = kept("ident", [P, P], F32)
         lme_sb = kept("lme_sb", [P, W], BF16)
         neg_lme = kept("neg_lme", [P, W], F32)
-        x_sb = [kept("x_sb%d" % i, [P, D], BF16) for i in range(W)]
+        vnorm_sb = kept("vnorm_sb", [P, N], BF16)
+        x_raw = [shared.tile([P, D], BF16, name="x_raw", tag="shared") for i in range(W)]
+        x_sorted = {i: kept("x_sorted%d" % i, [P, D // 2], F32) for i in range(1, W)}
         wq_raw = [kept("wq_raw%d" % g, [P, PACK, H], BF16) for g in range(D_PASSES)]
-        wq_codes = [kept("wq_codes%d" % g, [P, H], U32) for g in range(D_PASSES)]
-        wq_scale = [kept("wq_scale%d" % g, [P, H], U8) for g in range(D_PASSES)]
         u_raw = kept("u_raw", [P, L_PASSES, 2 * H], U8)
         u_scale_raw = kept("u_scale_raw", [P, L_PASSES, H], U8)
         u_codes = kept("u_codes", [P, L_PASSES, 2 * H], U8)
         u_scale = kept("u_scale", [P, L_PASSES, H], U8)
         c_codes = [kept("c_codes%d" % c, [P, L_PASSES, 2 * CHUNK], U8) for c in range(CHUNKS)]
         c_scale = kept("c_scale", [P, L_PASSES, N], U8)
-        key_codes = [kept("key_codes%d" % c, [P, CHUNK], U32) for c in range(CHUNKS)]
-        key_scale = [kept("key_scale%d" % c, [P, CHUNK], U8) for c in range(CHUNKS)]
+        wq_mx = [kept_operand("wq%d" % g, H) for g in range(D_PASSES)]
+        x_mx = [kept_operand("x%d" % i, D // PACK) for i in range(W)]
+        key_mx = [kept_operand("key%d" % c, CHUNK) for c in range(CHUNKS)]
+        query_mx = [kept_operand("query%d" % i, P) for i in range(W)]
         total = [kept("total%d" % c, [P, CHUNK], F32) for c in range(CHUNKS)]
-        vnorm_sb = kept("vnorm_sb", [P, N], BF16)
-
-        x_tiles = x.rearrange("(w i) d -> i w d", i=W)
-        u_scale_rows = u_scales.rearrange("g (q r) n -> r q g n", r=4)
-        c_scale_rows = c_scales.rearrange("g (q r) n -> r q g n", r=4)
+        x_turned, key_values, query_values, prob = {}, {}, {}, {}
 
         def load_x(i):
-            nc.sync.dma_start(out=x_sb[i][:], in_=x_tiles[i])
+            nc.sync.dma_start(out=x_raw[i][:], in_=x.rearrange("(w i) d -> i w d", i=W)[i])
 
         def load_wq(g):
             rows = wq[g * K_PASS : (g + 1) * K_PASS, :]
@@ -74,10 +86,13 @@ def tile_heavy_hitter_scores_s12_kernel(tc, x, wq, u_words, u_scales, c_words, c
             cols = c_words.rearrange("g p b -> p g b")[:, :, 2 * CHUNK * c : 2 * CHUNK * (c + 1)]
             nc.sync.dma_start(out=c_codes[c][:].bitcast(I32), in_=cols.bitcast(I32))
 
-        def load_scale_rows(queue, plane, rows, r):
-            queue.dma_start(out=plane[r:P:32, :, :].bitcast(I32), in_=rows[r].bitcast(I32))
+        def load_scales(plane, scales):
+            rows = scales.rearrange("g (q r) n -> r q g n", r=SCALE_ROWS)
+            for r in range(SCALE_ROWS):
+                nc.sync.dma_start(out=plane[r:P:32, :, :].bitcast(I32), in_=rows[r].bitcast(I32))
 
-        def quantize(codes, scales, values):
+        def quantize(operand, values):
+            codes, scales = operand
             nc.vector.quantize_mx(out=codes[:].bitcast(FP8X4), scales=scales[:], in_=values[:])
 
         def sort_u():
@@ -90,296 +105,208 @@ def tile_heavy_hitter_scores_s12_kernel(tc, x, wq, u_words, u_scales, c_words, c
                 in_=u_scale_raw[:].bitcast(I32).rearrange("p g (b t) -> p g t b", t=PACK),
             )
 
-        V, S = nc.vector.tensor_copy, nc.scalar.copy
-        held = {}
-
-        def group_wq(g, copy=V):
-            grouped = stage.tile([P, H * PACK], BF16, name="wq_grouped", align_bytes=64, bufs=2)
-            copy(
-                out=grouped[:].rearrange("p (t b i j) -> p t b j i", t=PACK, i=4, j=PACK),
-                in_=wq_raw[g][:].rearrange("p j (b t i) -> p t b j i", t=PACK, i=4),
+        def group_wq(g):
+            grouped = stage.tile([P, H * PACK], BF16, name="wq_grouped", align_bytes=64)
+            nc.vector.tensor_copy(
+                out=grouped[:].rearrange("p (t b r j) -> p t b j r", t=PACK, r=RUN, j=PACK),
+                in_=wq_raw[g][:].rearrange("p j (b t r) -> p t b j r", t=PACK, r=RUN),
             )
-            held["wq", g] = grouped
-
-        def quantize_wq(g):
-            quantize(wq_codes[g], wq_scale[g], held["wq", g])
+            return grouped
 
         def sort_x(i):
-            words = keep.tile([P, D // 2], F32, name="x_sorted%d" % i)
             nc.vector.tensor_copy(
-                out=words[:].rearrange("p (g u w) -> p g u w", g=D_PASSES, u=2),
-                in_=x_sb[i][:].bitcast(F32).rearrange("p (g w u) -> p g u w", g=D_PASSES, u=2),
+                out=x_sorted[i][:].rearrange("p (g u w) -> p g u w", g=D_PASSES, u=2),
+                in_=x_raw[i][:].bitcast(F32).rearrange("p (g w u) -> p g u w", g=D_PASSES, u=2),
             )
-            held["sorted", i] = words
 
-        def transpose_x(i):
-            held["x", i] = ahead.tile([P, D], BF16, name="x_grouped", align_bytes=64)
-            for half in range(2):
+        def transpose_x(i, copies):
+            x_turned[i] = turned.tile([P, D], BF16, name="x_turned", align_bytes=64)
+            for half, copy in enumerate(copies):
                 bank = new_bank()
                 for k in range(4):
                     g, u = 2 * half + k // 2, k % 2
-                    if ("sorted", i) in held:
-                        words = held["sorted", i][:, (2 * g + u) * P : (2 * g + u + 1) * P]
+                    if i in x_sorted:
+                        words = x_sorted[i][:, (2 * g + u) * P : (2 * g + u + 1) * P]
                     else:
-                        words = x_sb[i][:].bitcast(F32)[:, 256 * g + u : 256 * (g + 1) : 2]
+                        words = x_raw[i][:].bitcast(F32)[:, 2 * P * g + u : 2 * P * (g + 1) : 2]
                     nc.tensor.transpose(bank[:, k * P : (k + 1) * P], words, ident[:])
-                held["x_bank", i, half] = bank
+                target = x_turned[i][:].bitcast(F32)[:, half * CHUNK : (half + 1) * CHUNK]
+                copy(
+                    out=target.rearrange("p (g q u) -> p g q u", g=2, u=2),
+                    in_=bank[:].rearrange("p (g u q) -> p g q u", g=2, u=2),
+                )
 
-        def copy_x(i, half, copy):
-            half_words = D // 4
-            copy(
-                out=held["x", i][:].bitcast(F32)[:, half * half_words : (half + 1) * half_words].rearrange("p (g q u) -> p g q u", g=2, u=2),
-                in_=held["x_bank", i, half][:].rearrange("p (g u q) -> p g q u", g=2, u=2),
-            )
-
-        def quantize_x(i):
-            codes = ahead.tile([P, D // PACK], U32, name="x_codes", align_bytes=64)
-            scales = ahead.tile([P, D // PACK], U8, name="x_scale", align_bytes=64)
-            quantize(codes, scales, held["x", i])
-            held["x_operand", i] = codes, scales
-
-        def keys_piece(c, piece, copy=S):
-            if piece == 0:
-                held["keys", c] = stage.tile([P, CHUNK * PACK], BF16, name="key_grouped", align_bytes=64, bufs=2)
-            bank = new_bank()
-            n0 = c * CHUNK + piece * P
-            for t in range(PACK):
-                for g in range(L_PASSES):
-                    nc.tensor.matmul_mx(
-                        out=bank[:, t * P : (t + 1) * P],
-                        lhsT=u_codes[:, g, 2 * P * t : 2 * P * (t + 1)].bitcast(FP4X4),
-                        lhsT_scale=u_scale[:, g, P * t : P * (t + 1)],
-                        rhs=c_codes[c][:, g, 2 * P * piece : 2 * P * (piece + 1)].bitcast(FP4X4),
-                        rhs_scale=c_scale[:, g, n0 : n0 + P],
-                        start=(g == 0),
-                        stop=(g == L_PASSES - 1),
-                    )
-            copy(
-                out=held["keys", c][:, piece * K_PASS : (piece + 1) * K_PASS].rearrange("p (n t) -> p n t", t=PACK),
-                in_=bank[:].rearrange("p (t n) -> p n t", t=PACK),
-            )
-
-        def keys_chunk(c, copies=(S, S, S, S)):
+        def keys_chunk(c):
+            key_values[c] = stage.tile([P, CHUNK * PACK], BF16, name="key_values", align_bytes=64)
             for piece in range(CHUNK // P):
-                keys_piece(c, piece, copies[piece])
-
-        def quantize_keys(c):
-            quantize(key_codes[c], key_scale[c], held["keys", c])
+                bank = new_bank()
+                first_key = c * CHUNK + piece * P
+                for t in range(PACK):
+                    for g in range(L_PASSES):
+                        nc.tensor.matmul_mx(
+                            out=bank[:, t * P : (t + 1) * P],
+                            lhsT=u_codes[:, g, 2 * P * t : 2 * P * (t + 1)].bitcast(FP4X4),
+                            lhsT_scale=u_scale[:, g, P * t : P * (t + 1)],
+                            rhs=c_codes[c][:, g, 2 * P * piece : 2 * P * (piece + 1)].bitcast(FP4X4),
+                            rhs_scale=c_scale[:, g, first_key : first_key + P],
+                            start=(g == 0),
+                            stop=(g == L_PASSES - 1),
+                        )
+                nc.scalar.copy(
+                    out=key_values[c][:, piece * K_PASS : (piece + 1) * K_PASS].rearrange("p (n t) -> p n t", t=PACK),
+                    in_=bank[:].rearrange("p (t n) -> p n t", t=PACK),
+                )
 
         def query_tile(i, copy):
-            codes, scales = held["x_operand", i]
+            x_codes, x_scale = x_mx[i]
             bank = new_bank()
             for t in range(PACK):
                 for g in range(D_PASSES):
+                    wq_codes, wq_scale = wq_mx[g]
                     nc.tensor.matmul_mx(
                         out=bank[:, t * P : (t + 1) * P],
-                        lhsT=wq_codes[g][:, P * t : P * (t + 1)].bitcast(FP8X4),
-                        lhsT_scale=wq_scale[g][:, P * t : P * (t + 1)],
-                        rhs=codes[:, P * g : P * (g + 1)].bitcast(FP8X4),
-                        rhs_scale=scales[:, P * g : P * (g + 1)],
+                        lhsT=wq_codes[:, P * t : P * (t + 1)].bitcast(FP8X4),
+                        lhsT_scale=wq_scale[:, P * t : P * (t + 1)],
+                        rhs=x_codes[:, P * g : P * (g + 1)].bitcast(FP8X4),
+                        rhs_scale=x_scale[:, P * g : P * (g + 1)],
                         start=(g == 0),
                         stop=(g == D_PASSES - 1),
                     )
-            grouped = stage.tile([P, K_PASS], BF16, name="query_grouped", align_bytes=64)
+            query_values[i] = stage.tile([P, K_PASS], BF16, name="query_values", align_bytes=64)
             copy(
-                out=grouped[:].rearrange("p (q t) -> p q t", t=PACK),
+                out=query_values[i][:].rearrange("p (q t) -> p q t", t=PACK),
                 in_=bank[:].rearrange("p (t q) -> p q t", t=PACK),
             )
-            held["query", i] = grouped
-
-        def quantize_query(i):
-            codes = keep.tile([P, P], U32, name="query_codes%d" % i, align_bytes=64)
-            scales = keep.tile([P, P], U8, name="query_scale%d" % i, align_bytes=64)
-            quantize(codes, scales, held["query", i])
-            held["query_operand", i] = codes, scales
 
         def probabilities(i, c):
-            codes, scales = held["query_operand", i]
+            query_codes, query_scale = query_mx[i]
+            key_codes, key_scale = key_mx[c]
             bank = new_bank()
             nc.tensor.matmul_mx(
                 out=bank[:],
-                lhsT=codes[:].bitcast(FP8X4),
-                lhsT_scale=scales[:],
-                rhs=key_codes[c][:].bitcast(FP8X4),
-                rhs_scale=key_scale[c][:],
+                lhsT=query_codes[:].bitcast(FP8X4),
+                lhsT_scale=query_scale[:],
+                rhs=key_codes[:].bitcast(FP8X4),
+                rhs_scale=key_scale[:],
                 start=True,
                 stop=True,
             )
-            if i == 0:
-                nc.scalar.activation(out=total[c][:], in_=bank[:], func=ACT.Exp, bias=neg_lme[:, i : i + 1])
-                return
-            prob = probs.tile([P, CHUNK], F32, name="prob")
-            nc.scalar.activation(out=prob[:], in_=bank[:], func=ACT.Exp, bias=neg_lme[:, i : i + 1])
-            held["prob", i, c] = prob
+            if c == TENSOR_CHUNK:
+                prob[i, c] = shared.tile([P, CHUNK], F32, name="kept_prob", tag="shared")
+            elif i == 0:
+                prob[i, c] = total[c]
+            else:
+                prob[i, c] = probs.tile([P, CHUNK], F32, name="prob")
+            nc.scalar.activation(out=prob[i, c][:], in_=bank[:], func=ACT.Exp, bias=neg_lme[:, i : i + 1])
 
-        def add(i, c):
+        def add_on_vector(i, c):
             if i > 0:
-                nc.vector.tensor_tensor(out=total[c][:], in0=total[c][:], in1=held["prob", i, c][:], op=ALU.add)
+                nc.vector.tensor_tensor(out=total[c][:], in0=total[c][:], in1=prob[i, c][:], op=ALU.add)
 
-        def finish(c):
-            cols = slice(c * CHUNK, (c + 1) * CHUNK)
-            result = probs.tile([P, CHUNK], F32, name="result", bufs=4)
-            nc.vector.tensor_tensor(out=result[:], in0=total[c][:], in1=vnorm_sb[:, cols], op=ALU.mult)
+        def add_on_tensor(i, sum_bank):
+            for block in range(CHUNK // P):
+                cols = slice(block * P, (block + 1) * P)
+                nc.tensor.matmul(
+                    out=sum_bank[:, cols],
+                    lhsT=prob[i, TENSOR_CHUNK][:, cols],
+                    rhs=ident[:],
+                    is_transpose=True,
+                    start=(i == 0 and block == 0),
+                    stop=(i == W - 1 and block == CHUNK // P - 1),
+                )
+
+        def turn_back(half, sum_bank):
+            cols = slice(half * HALF, (half + 1) * HALF)
+            by_key = total[TENSOR_CHUNK][:, cols]
+            nc.scalar.copy(out=by_key, in_=sum_bank[:, cols])
+            bank = new_bank()
+            for block in range(HALF // P):
+                nc.tensor.transpose(bank[:, block * P : (block + 1) * P], by_key[:, block * P : (block + 1) * P], ident[:])
+            return bank[:, :HALF]
+
+        def finish(window_sums, first_key, width):
+            cols = slice(first_key, first_key + width)
+            result = keep.tile([P, width], F32, name="result%d" % first_key)
+            nc.vector.tensor_tensor(out=result[:], in0=window_sums, in1=vnorm_sb[:, cols], op=ALU.mult)
             nc.sync.dma_start(out=out[:, cols], in_=result[:])
+
+        def finish_chunk(c):
+            finish(total[c][:], c * CHUNK, CHUNK)
 
         nc.gpsimd.memset(u_scale_raw[:].bitcast(I32), 0)
         nc.vector.memset(c_scale[:].bitcast(I32), 0)
         make_identity(nc, ident[:])
         nc.sync.dma_start(out=lme_sb[:], in_=lme.rearrange("(w i) -> w i", i=W))
-        for r in range(4):
-            load_scale_rows(nc.sync, u_scale_raw, u_scale_rows, r)
-        load_scale_rows(nc.sync, c_scale, c_scale_rows, 0)
-        nc.sync.dma_start(out=u_raw[:].bitcast(I32), in_=u_words.rearrange("g p b -> p g b").bitcast(I32))
+        load_scales(u_scale_raw, u_scales)
         load_x(0)
-        for r in range(1, 4):
-            load_scale_rows(nc.sync, c_scale, c_scale_rows, r)
+        nc.sync.dma_start(out=u_raw[:].bitcast(I32), in_=u_words.rearrange("g p b -> p g b").bitcast(I32))
         load_c(0)
-        load_wq(0)
-        load_c(1)
-        load_wq(1)
-        load_c(2)
-        load_wq(2)
-        load_wq(3)
-        load_c(3)
-        load_x(1)
-        load_x(2)
-        load_x(3)
-        load_x(4)
-        load_x(5)
-        load_x(6)
-        load_x(7)
+        load_scales(c_scale, c_scales)
+        for g in range(D_PASSES):
+            load_wq(g)
+            if g + 1 < CHUNKS:
+                load_c(g + 1)
+            load_x(g + 1)
+        for i in SECOND_RUN:
+            load_x(i)
         nc.sync.dma_start(out=vnorm_sb[:], in_=vnorm.partition_broadcast(P))
+
         nc.scalar.activation(out=neg_lme[:], in_=lme_sb[:], func=ACT.Copy, scale=-1.0)
-        transpose_x(0)
-        copy_x(0, 0, S)
-        copy_x(0, 1, S)
+        transpose_x(0, (on_scalar, on_scalar))
         sort_u()
-        quantize_x(0)
-        keys_chunk(0)
-        group_wq(0, V)
-        group_wq(1, V)
-        quantize_wq(0)
-        keys_chunk(1)
-        quantize_wq(1)
-        group_wq(2, V)
-        quantize_keys(0)
-        quantize_wq(2)
-        keys_chunk(2)
-        group_wq(3, V)
-        quantize_keys(1)
-        quantize_wq(3)
-        transpose_x(1)
-        copy_x(1, 0, S)
-        copy_x(1, 1, S)
-        keys_chunk(3)
-        quantize_keys(2)
-        query_tile(0, V)
-        quantize_x(1)
-        quantize_keys(3)
-        quantize_query(0)
-        transpose_x(2)
-        copy_x(2, 0, S)
-        copy_x(2, 1, S)
-        query_tile(1, V)
-        quantize_x(2)
-        quantize_query(1)
-        probabilities(0, 0)
-        add(0, 0)
-        probabilities(0, 1)
-        add(0, 1)
-        probabilities(0, 2)
-        add(0, 2)
-        probabilities(0, 3)
-        add(0, 3)
-        transpose_x(3)
-        copy_x(3, 0, S)
-        copy_x(3, 1, S)
-        query_tile(2, V)
-        quantize_x(3)
-        quantize_query(2)
-        probabilities(1, 0)
-        add(1, 0)
-        probabilities(1, 1)
-        add(1, 1)
-        probabilities(1, 2)
-        add(1, 2)
-        probabilities(1, 3)
-        add(1, 3)
-        transpose_x(4)
-        copy_x(4, 0, S)
-        copy_x(4, 1, S)
-        query_tile(3, V)
-        quantize_x(4)
-        quantize_query(3)
-        probabilities(2, 0)
-        add(2, 0)
-        probabilities(2, 1)
-        add(2, 1)
-        probabilities(2, 2)
-        add(2, 2)
-        probabilities(2, 3)
-        add(2, 3)
-        transpose_x(5)
-        copy_x(5, 0, S)
-        copy_x(5, 1, S)
-        query_tile(4, V)
-        quantize_x(5)
-        quantize_query(4)
-        probabilities(3, 0)
-        add(3, 0)
-        probabilities(3, 1)
-        add(3, 1)
-        probabilities(3, 2)
-        add(3, 2)
-        probabilities(3, 3)
-        add(3, 3)
-        transpose_x(6)
-        copy_x(6, 0, S)
-        copy_x(6, 1, S)
-        query_tile(5, V)
-        quantize_x(6)
-        quantize_query(5)
-        probabilities(4, 0)
-        add(4, 0)
-        probabilities(4, 1)
-        add(4, 1)
-        probabilities(4, 2)
-        add(4, 2)
-        probabilities(4, 3)
-        add(4, 3)
-        transpose_x(7)
-        copy_x(7, 0, S)
-        copy_x(7, 1, S)
-        query_tile(6, V)
-        quantize_x(7)
-        quantize_query(6)
-        probabilities(5, 0)
-        add(5, 0)
-        probabilities(5, 1)
-        add(5, 1)
-        probabilities(5, 2)
-        add(5, 2)
-        probabilities(5, 3)
-        add(5, 3)
-        query_tile(7, S)
-        quantize_query(7)
-        probabilities(6, 0)
-        add(6, 0)
-        probabilities(6, 1)
-        add(6, 1)
-        probabilities(6, 2)
-        add(6, 2)
-        probabilities(6, 3)
-        add(6, 3)
-        probabilities(7, 0)
-        add(7, 0)
-        probabilities(7, 1)
-        add(7, 1)
-        finish(0)
-        probabilities(7, 2)
-        add(7, 2)
-        finish(1)
-        probabilities(7, 3)
-        add(7, 3)
-        finish(2)
-        finish(3)
+        quantize(x_mx[0], x_turned[0])
+        for c in range(CHUNKS):
+            keys_chunk(c)
+            wq_grouped = group_wq(c)
+            if c > 0:
+                quantize(key_mx[c - 1], key_values[c - 1])
+            quantize(wq_mx[c], wq_grouped)
+            sort_x(c + 1)
+
+        for i in FIRST_RUN:
+            transpose_x(i, (on_scalar, on_vector if i == 1 else on_scalar))
+        quantize(key_mx[CHUNKS - 1], key_values[CHUNKS - 1])
+        quantize(x_mx[1], x_turned[1])
+        sort_x(5)
+        sort_x(6)
+        query_tile(0, on_scalar)
+        quantize(x_mx[2], x_turned[2])
+        quantize(query_mx[0], query_values[0])
+        sort_x(7)
+        query_tile(1, on_scalar)
+        quantize(x_mx[3], x_turned[3])
+        quantize(query_mx[1], query_values[1])
+        quantize(x_mx[4], x_turned[4])
+        for i in SECOND_RUN:
+            transpose_x(i, (on_scalar, on_vector))
+        for i in SECOND_RUN:
+            quantize(x_mx[i], x_turned[i])
+
+        for i in range(W - LEAD):
+            for c in range(CHUNKS):
+                probabilities(i, c)
+            add_on_vector(i, 0)
+            add_on_vector(i, 1)
+            query_tile(i + LEAD, on_vector)
+            add_on_vector(i, 2)
+            quantize(query_mx[i + LEAD], query_values[i + LEAD])
+
+        sum_bank = sum_pool.tile([P, CHUNK], F32, name="sum_bank")
+        for c in range(CHUNKS):
+            probabilities(W - 2, c)
+        for c in range(TENSOR_CHUNK):
+            add_on_vector(W - 2, c)
+        for i in range(EARLY_SUMS):
+            add_on_tensor(i, sum_bank)
+        for c in range(CHUNKS):
+            probabilities(W - 1, c)
+        for c in range(TENSOR_CHUNK):
+            add_on_vector(W - 1, c)
+            if c > 0:
+                finish_chunk(c - 1)
+        finish_chunk(TENSOR_CHUNK - 1)
+        for i in range(EARLY_SUMS, W):
+            add_on_tensor(i, sum_bank)
+        halves = [turn_back(half, sum_bank) for half in range(2)]
+        for half in range(2):
+            finish(halves[half], TENSOR_CHUNK * CHUNK + half * HALF, HALF)

@@ -27,8 +27,6 @@ CHUNKS = N // CHUNK
 HALF = CHUNK // 2
 SCALE_ROWS = 4
 TENSOR_CHUNK = CHUNKS - 1
-FIRST_RUN = range(1, 5)
-SECOND_RUN = range(5, W)
 LEAD = 2
 EARLY_SUMS = 2
 
@@ -56,6 +54,7 @@ def tile_heavy_hitter_scores_s12_kernel(tc, x, wq, u_words, u_scales, c_words, c
             return psum.tile([P, CHUNK], F32, name="bank")
 
         ident = kept("ident", [P, P], F32)
+        zeros = kept("zeros", [P, CHUNK], BF16)
         lme_sb = kept("lme_sb", [P, W], BF16)
         neg_lme = kept("neg_lme", [P, W], F32)
         vnorm_sb = kept("vnorm_sb", [P, N], BF16)
@@ -115,8 +114,8 @@ def tile_heavy_hitter_scores_s12_kernel(tc, x, wq, u_words, u_scales, c_words, c
 
         def sort_x(i):
             nc.vector.tensor_copy(
-                out=x_sorted[i][:].rearrange("p (g u w) -> p g u w", g=D_PASSES, u=2),
-                in_=x_raw[i][:].bitcast(F32).rearrange("p (g w u) -> p g u w", g=D_PASSES, u=2),
+                out=x_sorted[i][:].rearrange("p (g u w) -> p g w u", g=D_PASSES, u=2),
+                in_=x_raw[i][:].bitcast(F32).rearrange("p (g w u) -> p g w u", g=D_PASSES, u=2),
             )
 
         def transpose_x(i, copies):
@@ -233,54 +232,73 @@ def tile_heavy_hitter_scores_s12_kernel(tc, x, wq, u_words, u_scales, c_words, c
         def finish_chunk(c):
             finish(total[c][:], c * CHUNK, CHUNK)
 
+        def warm_up(count, moving):
+            bank = new_bank()
+            for k in range(count):
+                nc.tensor.matmul(out=bank[:], lhsT=zeros[:, :P], rhs=moving, start=True, stop=True)
+
         nc.gpsimd.memset(u_scale_raw[:].bitcast(I32), 0)
         nc.vector.memset(c_scale[:].bitcast(I32), 0)
+        nc.vector.memset(zeros[:], 0.0)
         make_identity(nc, ident[:])
         nc.sync.dma_start(out=lme_sb[:], in_=lme.rearrange("(w i) -> w i", i=W))
+        load_wq(0)
         load_scales(u_scale_raw, u_scales)
         load_x(0)
         nc.sync.dma_start(out=u_raw[:].bitcast(I32), in_=u_words.rearrange("g p b -> p g b").bitcast(I32))
         load_c(0)
         load_scales(c_scale, c_scales)
-        for g in range(D_PASSES):
+        for g in range(1, D_PASSES):
             load_wq(g)
-            if g + 1 < CHUNKS:
-                load_c(g + 1)
-            load_x(g + 1)
-        for i in SECOND_RUN:
+            load_c(g)
+            load_x(g)
+        for i in range(D_PASSES, W):
             load_x(i)
         nc.sync.dma_start(out=vnorm_sb[:], in_=vnorm.partition_broadcast(P))
 
         nc.scalar.activation(out=neg_lme[:], in_=lme_sb[:], func=ACT.Copy, scale=-1.0)
+        warm_up(4, zeros[:])
+        warm_up(2, wq_raw[0][:, 0, :])
+        wq_grouped = group_wq(0)
         transpose_x(0, (on_scalar, on_scalar))
+        warm_up(2, zeros[:])
+        quantize(wq_mx[0], wq_grouped)
         sort_u()
         quantize(x_mx[0], x_turned[0])
-        for c in range(CHUNKS):
+
+        for c in range(CHUNKS - 1):
             keys_chunk(c)
-            wq_grouped = group_wq(c)
+            wq_grouped = group_wq(c + 1)
             if c > 0:
                 quantize(key_mx[c - 1], key_values[c - 1])
-            quantize(wq_mx[c], wq_grouped)
+            quantize(wq_mx[c + 1], wq_grouped)
             sort_x(c + 1)
 
-        for i in FIRST_RUN:
-            transpose_x(i, (on_scalar, on_vector if i == 1 else on_scalar))
-        quantize(key_mx[CHUNKS - 1], key_values[CHUNKS - 1])
-        quantize(x_mx[1], x_turned[1])
+        for i in (1, 2):
+            transpose_x(i, (on_scalar, on_scalar))
+        keys_chunk(CHUNKS - 1)
+        sort_x(4)
+        quantize(key_mx[CHUNKS - 2], key_values[CHUNKS - 2])
         sort_x(5)
+        quantize(x_mx[1], x_turned[1])
         sort_x(6)
-        query_tile(0, on_scalar)
-        quantize(x_mx[2], x_turned[2])
-        quantize(query_mx[0], query_values[0])
         sort_x(7)
-        query_tile(1, on_scalar)
+        for i in (3, 4):
+            transpose_x(i, (on_scalar, on_scalar))
+        quantize(key_mx[CHUNKS - 1], key_values[CHUNKS - 1])
+        quantize(x_mx[2], x_turned[2])
+        query_tile(0, on_scalar)
         quantize(x_mx[3], x_turned[3])
-        quantize(query_mx[1], query_values[1])
-        quantize(x_mx[4], x_turned[4])
-        for i in SECOND_RUN:
+        quantize(query_mx[0], query_values[0])
+        for i in (5, 6):
             transpose_x(i, (on_scalar, on_vector))
-        for i in SECOND_RUN:
-            quantize(x_mx[i], x_turned[i])
+        quantize(x_mx[4], x_turned[4])
+        query_tile(1, on_scalar)
+        quantize(x_mx[5], x_turned[5])
+        quantize(query_mx[1], query_values[1])
+        transpose_x(7, (on_scalar, on_vector))
+        quantize(x_mx[6], x_turned[6])
+        quantize(x_mx[7], x_turned[7])
 
         for i in range(W - LEAD):
             for c in range(CHUNKS):
@@ -296,17 +314,18 @@ def tile_heavy_hitter_scores_s12_kernel(tc, x, wq, u_words, u_scales, c_words, c
             probabilities(W - 2, c)
         for c in range(TENSOR_CHUNK):
             add_on_vector(W - 2, c)
-        for i in range(EARLY_SUMS):
+        for pair in range(CHUNKS // 2):
+            for i in range(pair * EARLY_SUMS, (pair + 1) * EARLY_SUMS):
+                add_on_tensor(i, sum_bank)
+            probabilities(W - 1, 2 * pair)
+            probabilities(W - 1, 2 * pair + 1)
+        for i in range(CHUNKS // 2 * EARLY_SUMS, W):
             add_on_tensor(i, sum_bank)
-        for c in range(CHUNKS):
-            probabilities(W - 1, c)
         for c in range(TENSOR_CHUNK):
             add_on_vector(W - 1, c)
             if c > 0:
                 finish_chunk(c - 1)
         finish_chunk(TENSOR_CHUNK - 1)
-        for i in range(EARLY_SUMS, W):
-            add_on_tensor(i, sum_bank)
         halves = [turn_back(half, sum_bank) for half in range(2)]
         for half in range(2):
             finish(halves[half], TENSOR_CHUNK * CHUNK + half * HALF, HALF)

@@ -54,7 +54,6 @@ def tile_heavy_hitter_scores_s12_kernel(tc, x, wq, u_words, u_scales, c_words, c
             return psum.tile([P, CHUNK], F32, name="bank")
 
         ident = kept("ident", [P, P], F32)
-        zeros = kept("zeros", [P, CHUNK], BF16)
         lme_sb = kept("lme_sb", [P, W], BF16)
         neg_lme = kept("neg_lme", [P, W], F32)
         vnorm_sb = kept("vnorm_sb", [P, N], BF16)
@@ -232,14 +231,8 @@ def tile_heavy_hitter_scores_s12_kernel(tc, x, wq, u_words, u_scales, c_words, c
         def finish_chunk(c):
             finish(total[c][:], c * CHUNK, CHUNK)
 
-        def warm_up(count, moving):
-            bank = new_bank()
-            for k in range(count):
-                nc.tensor.matmul(out=bank[:], lhsT=zeros[:, :P], rhs=moving, start=True, stop=True)
-
         nc.gpsimd.memset(u_scale_raw[:].bitcast(I32), 0)
         nc.vector.memset(c_scale[:].bitcast(I32), 0)
-        nc.vector.memset(zeros[:], 0.0)
         make_identity(nc, ident[:])
         nc.sync.dma_start(out=lme_sb[:], in_=lme.rearrange("(w i) -> w i", i=W))
         load_wq(0)
@@ -257,11 +250,8 @@ def tile_heavy_hitter_scores_s12_kernel(tc, x, wq, u_words, u_scales, c_words, c
         nc.sync.dma_start(out=vnorm_sb[:], in_=vnorm.partition_broadcast(P))
 
         nc.scalar.activation(out=neg_lme[:], in_=lme_sb[:], func=ACT.Copy, scale=-1.0)
-        warm_up(4, zeros[:])
-        warm_up(2, wq_raw[0][:, 0, :])
         wq_grouped = group_wq(0)
         transpose_x(0, (on_scalar, on_scalar))
-        warm_up(2, zeros[:])
         quantize(wq_mx[0], wq_grouped)
         sort_u()
         quantize(x_mx[0], x_turned[0])

from contextlib import ExitStack

import concourse.mybir as mybir
from concourse.masks import make_identity

M, D, L, H, N, W = 1024, 2048, 1024, 512, 2048, 8
FLOPS = 2 * (M * D * H + H * L * N + M * H * N)

F32 = mybir.dt.float32
BF16 = mybir.dt.bfloat16
I32 = mybir.dt.int32
U32 = mybir.dt.uint32
U8 = mybir.dt.uint8
FP8X4 = mybir.dt.float8_e4m3fn_x4
FP4X4 = mybir.dt.float4_e2m1fn_x4
ACT = mybir.ActivationFunctionType
ALU = mybir.AluOpType

P = 128
PACK = 4
RUN = 4
K_PASS = P * PACK
D_PASSES = D // K_PASS
L_PASSES = L // K_PASS
CHUNK = 512
CHUNKS = N // CHUNK
HALF = CHUNK // 2
SCALE_ROWS = 4
TENSOR_CHUNK = CHUNKS - 1
LEAD = 2
EARLY_SUMS = 2


def tile_heavy_hitter_scores_s12_kernel(tc, x, wq, u_words, u_scales, c_words, c_scales, lme, vnorm, out):
    nc = tc.nc
    on_vector, on_scalar = nc.vector.tensor_copy, nc.scalar.copy
    with ExitStack() as ctx:
        keep = ctx.enter_context(tc.tile_pool(name="keep", bufs=1))
        shared = ctx.enter_context(tc.tile_pool(name="shared", bufs=W))
        stage = ctx.enter_context(tc.tile_pool(name="stage", bufs=2))
        turned = ctx.enter_context(tc.tile_pool(name="turned", bufs=6))
        probs = ctx.enter_context(tc.tile_pool(name="probs", bufs=5))
        psum = ctx.enter_context(tc.psum_pool(name="psum", bufs=7))
        sum_pool = ctx.enter_context(tc.psum_pool(name="sum_pool", bufs=1))
        ctx.enter_context(tc.manual_schedule())

        def kept(name, shape, dtype):
            return keep.tile(shape, dtype, name=name, align_bytes=64)

        def kept_operand(name, columns):
            return kept(name + "_codes", [P, columns], U32), kept(name + "_scale", [P, columns], U8)

        def new_bank():
            return psum.tile([P, CHUNK], F32, name="bank")

        ident = kept("ident", [P, P], F32)
        lme_sb = kept("lme_sb", [P, W], BF16)
        neg_lme = kept("neg_lme", [P, W], F32)
        vnorm_sb = kept("vnorm_sb", [P, N], BF16)
        x_raw = [shared.tile([P, D], BF16, name="x_raw", tag="shared") for i in range(W)]
        x_sorted = {i: kept("x_sorted%d" % i, [P, D // 2], F32) for i in range(1, W)}
        wq_raw = [kept("wq_raw%d" % g, [P, PACK, H], BF16) for g in range(D_PASSES)]
        u_raw = kept("u_raw", [P, L_PASSES, 2 * H], U8)
        u_scale_raw = kept("u_scale_raw", [P, L_PASSES, H], U8)
        u_codes = kept("u_codes", [P, L_PASSES, 2 * H], U8)
        u_scale = kept("u_scale", [P, L_PASSES, H], U8)
        c_codes = [kept("c_codes%d" % c, [P, L_PASSES, 2 * CHUNK], U8) for c in range(CHUNKS)]
        c_scale = kept("c_scale", [P, L_PASSES, N], U8)
        wq_mx = [kept_operand("wq%d" % g, H) for g in range(D_PASSES)]
        x_mx = [kept_operand("x%d" % i, D // PACK) for i in range(W)]
        key_mx = [kept_operand("key%d" % c, CHUNK) for c in range(CHUNKS)]
        query_mx = [kept_operand("query%d" % i, P) for i in range(W)]
        total = [kept("total%d" % c, [P, CHUNK], F32) for c in range(CHUNKS)]
        x_turned, key_values, query_values, prob = {}, {}, {}, {}

        def load_x(i):
            nc.sync.dma_start(out=x_raw[i][:], in_=x.rearrange("(w i) d -> i w d", i=W)[i])

        def load_wq(g):
            rows = wq[g * K_PASS : (g + 1) * K_PASS, :]
            nc.sync.dma_start(out=wq_raw[g][:], in_=rows.rearrange("(p j) h -> p j h", j=PACK))

        def load_c(c):
            cols = c_words.rearrange("g p b -> p g b")[:, :, 2 * CHUNK * c : 2 * CHUNK * (c + 1)]
            nc.sync.dma_start(out=c_codes[c][:].bitcast(I32), in_=cols.bitcast(I32))

        def load_scales(plane, scales):
            rows = scales.rearrange("g (q r) n -> r q g n", r=SCALE_ROWS)
            for r in range(SCALE_ROWS):
                nc.sync.dma_start(out=plane[r:P:32, :, :].bitcast(I32), in_=rows[r].bitcast(I32))

        def quantize(operand, values):
            codes, scales = operand
            nc.vector.quantize_mx(out=codes[:].bitcast(FP8X4), scales=scales[:], in_=values[:])

        def sort_u():
            nc.vector.tensor_copy(
                out=u_codes[:].bitcast(I32).rearrange("p g (t b w) -> p g t b w", t=PACK, w=2),
                in_=u_raw[:].bitcast(I32).rearrange("p g (b t w) -> p g t b w", t=PACK, w=2),
            )
            nc.vector.tensor_copy(
                out=u_scale[:].bitcast(I32).rearrange("p g (t b) -> p g t b", t=PACK),
                in_=u_scale_raw[:].bitcast(I32).rearrange("p g (b t) -> p g t b", t=PACK),
            )

        def group_wq(g):
            grouped = stage.tile([P, H * PACK], BF16, name="wq_grouped", align_bytes=64)
            nc.vector.tensor_copy(
                out=grouped[:].rearrange("p (t b r j) -> p t b j r", t=PACK, r=RUN, j=PACK),
                in_=wq_raw[g][:].rearrange("p j (b t r) -> p t b j r", t=PACK, r=RUN),
            )
            return grouped

        def sort_x(i):
            nc.vector.tensor_copy(
                out=x_sorted[i][:].rearrange("p (g u w) -> p g w u", g=D_PASSES, u=2),
                in_=x_raw[i][:].bitcast(F32).rearrange("p (g w u) -> p g w u", g=D_PASSES, u=2),
            )

        def transpose_x(i, copies):
            x_turned[i] = turned.tile([P, D], BF16, name="x_turned", align_bytes=64)
            for half, copy in enumerate(copies):
                bank = new_bank()
                for k in range(4):
                    g, u = 2 * half + k // 2, k % 2
                    if i in x_sorted:
                        words = x_sorted[i][:, (2 * g + u) * P : (2 * g + u + 1) * P]
                    else:
                        words = x_raw[i][:].bitcast(F32)[:, 2 * P * g + u : 2 * P * (g + 1) : 2]
                    nc.tensor.transpose(bank[:, k * P : (k + 1) * P], words, ident[:])
                target = x_turned[i][:].bitcast(F32)[:, half * CHUNK : (half + 1) * CHUNK]
                copy(
                    out=target.rearrange("p (g q u) -> p g q u", g=2, u=2),
                    in_=bank[:].rearrange("p (g u q) -> p g q u", g=2, u=2),
                )

        def keys_chunk(c):
            key_values[c] = stage.tile([P, CHUNK * PACK], BF16, name="key_values", align_bytes=64)
            for piece in range(CHUNK // P):
                bank = new_bank()
                first_key = c * CHUNK + piece * P
                for t in range(PACK):
                    for g in range(L_PASSES):
                        nc.tensor.matmul_mx(
                            out=bank[:, t * P : (t + 1) * P],
                            lhsT=u_codes[:, g, 2 * P * t : 2 * P * (t + 1)].bitcast(FP4X4),
                            lhsT_scale=u_scale[:, g, P * t : P * (t + 1)],
                            rhs=c_codes[c][:, g, 2 * P * piece : 2 * P * (piece + 1)].bitcast(FP4X4),
                            rhs_scale=c_scale[:, g, first_key : first_key + P],
                            start=(g == 0),
                            stop=(g == L_PASSES - 1),
                        )
                nc.scalar.copy(
                    out=key_values[c][:, piece * K_PASS : (piece + 1) * K_PASS].rearrange("p (n t) -> p n t", t=PACK),
                    in_=bank[:].rearrange("p (t n) -> p n t", t=PACK),
                )

        def query_tile(i, copy):
            x_codes, x_scale = x_mx[i]
            bank = new_bank()
            for t in range(PACK):
                for g in range(D_PASSES):
                    wq_codes, wq_scale = wq_mx[g]
                    nc.tensor.matmul_mx(
                        out=bank[:, t * P : (t + 1) * P],
                        lhsT=wq_codes[:, P * t : P * (t + 1)].bitcast(FP8X4),
                        lhsT_scale=wq_scale[:, P * t : P * (t + 1)],
                        rhs=x_codes[:, P * g : P * (g + 1)].bitcast(FP8X4),
                        rhs_scale=x_scale[:, P * g : P * (g + 1)],
                        start=(g == 0),
                        stop=(g == D_PASSES - 1),
                    )
            query_values[i] = stage.tile([P, K_PASS], BF16, name="query_values", align_bytes=64)
            copy(
                out=query_values[i][:].rearrange("p (q t) -> p q t", t=PACK),
                in_=bank[:].rearrange("p (t q) -> p q t", t=PACK),
            )

        def probabilities(i, c):
            query_codes, query_scale = query_mx[i]
            key_codes, key_scale = key_mx[c]
            bank = new_bank()
            nc.tensor.matmul_mx(
                out=bank[:],
                lhsT=query_codes[:].bitcast(FP8X4),
                lhsT_scale=query_scale[:],
                rhs=key_codes[:].bitcast(FP8X4),
                rhs_scale=key_scale[:],
                start=True,
                stop=True,
            )
            if c == TENSOR_CHUNK:
                prob[i, c] = shared.tile([P, CHUNK], F32, name="kept_prob", tag="shared")
            elif i == 0:
                prob[i, c] = total[c]
            else:
                prob[i, c] = probs.tile([P, CHUNK], F32, name="prob")
            nc.scalar.activation(out=prob[i, c][:], in_=bank[:], func=ACT.Exp, bias=neg_lme[:, i : i + 1])

        def add_on_vector(i, c):
            if i > 0:
                nc.vector.tensor_tensor(out=total[c][:], in0=total[c][:], in1=prob[i, c][:], op=ALU.add)

        def add_on_tensor(i, sum_bank):
            for block in range(CHUNK // P):
                cols = slice(block * P, (block + 1) * P)
                nc.tensor.matmul(
                    out=sum_bank[:, cols],
                    lhsT=prob[i, TENSOR_CHUNK][:, cols],
                    rhs=ident[:],
                    is_transpose=True,
                    start=(i == 0 and block == 0),
                    stop=(i == W - 1 and block == CHUNK // P - 1),
                )

        def turn_back(half, sum_bank):
            cols = slice(half * HALF, (half + 1) * HALF)
            by_key = total[TENSOR_CHUNK][:, cols]
            nc.scalar.copy(out=by_key, in_=sum_bank[:, cols])
            bank = new_bank()
            for block in range(HALF // P):
                nc.tensor.transpose(bank[:, block * P : (block + 1) * P], by_key[:, block * P : (block + 1) * P], ident[:])
            return bank[:, :HALF]

        def finish(window_sums, first_key, width):
            cols = slice(first_key, first_key + width)
            result = keep.tile([P, width], F32, name="result%d" % first_key)
            nc.vector.tensor_tensor(out=result[:], in0=window_sums, in1=vnorm_sb[:, cols], op=ALU.mult)
            nc.sync.dma_start(out=out[:, cols], in_=result[:])

        def finish_chunk(c):
            finish(total[c][:], c * CHUNK, CHUNK)

        nc.gpsimd.memset(u_scale_raw[:].bitcast(I32), 0)
        nc.vector.memset(c_scale[:].bitcast(I32), 0)
        make_identity(nc, ident[:])
        nc.sync.dma_start(out=lme_sb[:], in_=lme.rearrange("(w i) -> w i", i=W))
        load_wq(0)
        load_scales(u_scale_raw, u_scales)
        load_x(0)
        nc.sync.dma_start(out=u_raw[:].bitcast(I32), in_=u_words.rearrange("g p b -> p g b").bitcast(I32))
        load_c(0)
        load_scales(c_scale, c_scales)
        for g in range(1, D_PASSES):
            load_wq(g)
            load_c(g)
            load_x(g)
        for i in range(D_PASSES, W):
            load_x(i)
        nc.sync.dma_start(out=vnorm_sb[:], in_=vnorm.partition_broadcast(P))

        nc.scalar.activation(out=neg_lme[:], in_=lme_sb[:], func=ACT.Copy, scale=-1.0)
        wq_grouped = group_wq(0)
        transpose_x(0, (on_scalar, on_scalar))
        quantize(wq_mx[0], wq_grouped)
        sort_u()
        quantize(x_mx[0], x_turned[0])

        for c in range(CHUNKS - 1):
            keys_chunk(c)
            wq_grouped = group_wq(c + 1)
            if c > 0:
                quantize(key_mx[c - 1], key_values[c - 1])
            quantize(wq_mx[c + 1], wq_grouped)
            sort_x(c + 1)

        for i in (1, 2):
            transpose_x(i, (on_scalar, on_scalar))
        keys_chunk(CHUNKS - 1)
        sort_x(4)
        quantize(key_mx[CHUNKS - 2], key_values[CHUNKS - 2])
        sort_x(5)
        quantize(x_mx[1], x_turned[1])
        sort_x(6)
        sort_x(7)
        for i in (3, 4):
            transpose_x(i, (on_scalar, on_scalar))
        quantize(key_mx[CHUNKS - 1], key_values[CHUNKS - 1])
        quantize(x_mx[2], x_turned[2])
        query_tile(0, on_scalar)
        quantize(x_mx[3], x_turned[3])
        quantize(query_mx[0], query_values[0])
        for i in (5, 6):
            transpose_x(i, (on_scalar, on_vector))
        quantize(x_mx[4], x_turned[4])
        query_tile(1, on_scalar)
        quantize(x_mx[5], x_turned[5])
        quantize(query_mx[1], query_values[1])
        transpose_x(7, (on_scalar, on_vector))
        quantize(x_mx[6], x_turned[6])
        quantize(x_mx[7], x_turned[7])

        for i in range(W - LEAD):
            for c in range(CHUNKS):
                probabilities(i, c)
            add_on_vector(i, 0)
            add_on_vector(i, 1)
            query_tile(i + LEAD, on_vector)
            add_on_vector(i, 2)
            quantize(query_mx[i + LEAD], query_values[i + LEAD])

        sum_bank = sum_pool.tile([P, CHUNK], F32, name="sum_bank")
        for c in range(CHUNKS):
            probabilities(W - 2, c)
        for c in range(TENSOR_CHUNK):
            add_on_vector(W - 2, c)
        for pair in range(CHUNKS // 2):
            for i in range(pair * EARLY_SUMS, (pair + 1) * EARLY_SUMS):
                add_on_tensor(i, sum_bank)
            probabilities(W - 1, 2 * pair)
            probabilities(W - 1, 2 * pair + 1)
        for i in range(CHUNKS // 2 * EARLY_SUMS, W):
            add_on_tensor(i, sum_bank)
        for c in range(TENSOR_CHUNK):
            add_on_vector(W - 1, c)
            if c > 0:
                finish_chunk(c - 1)
        finish_chunk(TENSOR_CHUNK - 1)
        halves = [turn_back(half, sum_bank) for half in range(2)]
        for half in range(2):
            finish(halves[half], TENSOR_CHUNK * CHUNK + half * HALF, HALF)
